import numpy as np
import ml_dtypes


def mxq(x, axis, fmt="e4m3"):
    dtype, down = {"e4m3": (ml_dtypes.float8_e4m3fn, 7), "e5m2": (ml_dtypes.float8_e5m2, 14)}[fmt]
    v = np.moveaxis(np.asarray(x, np.float32).astype(ml_dtypes.bfloat16).astype(np.float64), axis, -1)
    blocks = v.reshape(v.shape[:-1] + (-1, 32))
    amax = np.abs(blocks).max(-1, keepdims=True)
    byte = np.maximum(np.where(amax > 0, np.frexp(amax)[1] - 1 + 127, 0) - down, 1)
    scale = np.exp2(byte - 127.0)
    codes = (blocks / scale).astype(np.float32).astype(dtype).astype(np.float64)
    return np.moveaxis((codes * scale).reshape(v.shape), -1, axis)


WIDE = False


def mx_kscale(k):
    if not WIDE:
        return np.ones(k)
    levels = np.array([10, -10, 5, -5, 0])
    if k % 512:
        return np.exp2(np.random.permutation(np.resize(levels, k // 32))).repeat(32)
    a = np.empty((k // 512, 16))
    for p in range(k // 512):
        a[p, :8] = np.random.permutation(np.resize(levels, 8))
        for g in range(8):
            far = levels[np.abs(levels - a[p, g]) >= 10]
            a[p, g + 8] = far[np.random.randint(len(far))]
    return np.exp2(a.ravel()).repeat(32)


def f64(x):
    return np.asarray(x).astype(np.float64)


def striped(idx):
    return np.tile(idx.reshape(-1, 16).T, (8, 1)).astype(np.uint16)


def unstriped(offs):
    return offs[:16].T.reshape(-1).astype(np.int64)


E2M1 = np.array([0.0, 0.5, 1.0, 1.5, 2.0, 3.0, 4.0, 6.0, -0.0, -0.5, -1.0, -1.5, -2.0, -3.0, -4.0, -6.0])


def pack_weight(w, fmt):
    k, n = w.shape
    w = f64(np.asarray(w, np.float32).astype(ml_dtypes.bfloat16)).reshape(k // 32, 32, n)
    amax = np.abs(w).max(1)
    if fmt == "e4m3":
        byte = np.frexp(amax)[1] - 1 + 127 - 7
    else:
        mant, ex = np.frexp(amax / 6.0)
        byte = np.where(mant > 0.5, ex, ex - 1) + 127
    byte = np.clip(np.where(amax > 0, byte, 1), 1, 254)
    scaled = (w * np.exp2(127.0 - byte)[:, None, :]).reshape(k, n).astype(np.float32)
    by_word = np.ascontiguousarray(scaled.reshape(k // 512, 128, 4, n).transpose(0, 1, 3, 2))
    if fmt == "e4m3":
        words = by_word.astype(ml_dtypes.float8_e4m3fn).view(np.uint8)
    else:
        c = by_word.astype(ml_dtypes.float4_e2m1fn).view(np.uint8) & 0xF
        words = (c[..., 0::2] | (c[..., 1::2] << 4)).reshape(k // 512, 128, 2 * n)
    return np.ascontiguousarray(words), np.ascontiguousarray(byte.astype(np.uint8).reshape(k // 512, 16, n))


def unpack_weight(words, scales, fmt):
    g, _, n = scales.shape
    words = np.ascontiguousarray(words).reshape(g, 128, n, -1)
    if fmt == "e4m3":
        vals = words.view(ml_dtypes.float8_e4m3fn).astype(np.float64)
    else:
        nib = np.empty((g, 128, n, 4), np.uint8)
        nib[..., 0::2] = words & 0xF
        nib[..., 1::2] = words >> 4
        vals = E2M1[nib]
    vals = vals * np.repeat(np.exp2(scales.astype(np.float64) - 127.0), 8, axis=1)[..., None]
    return vals.transpose(0, 1, 3, 2).reshape(g * 512, n)


def gelu(v):
    return 0.5 * v * (1.0 + np.tanh(np.sqrt(2.0 / np.pi) * (v + 0.044715 * v**3)))


K, H, T, S, T2, P = 1024, 512, 2048, 1024, 2048, 1024

def setup_inputs():
    n = np.random.standard_normal
    s = mx_kscale(K)[:, None]
    u = mx_kscale(H)[:, None]
    tab_words, tab_scales = pack_weight(n((K, T)) * s, "e4m3")
    w2_words, w2_scales = pack_weight(1.5 * n((K, H)) / s / np.sqrt(K), "e2m1")
    wb_words, wb_scales = pack_weight(n((H, H)) / u * u.T / np.sqrt(H), "e2m1")
    return {
        "tab_words": tab_words, "tab_scales": tab_scales,
        "offs": striped(np.random.permutation(T)[:S]),
        "offs2": striped(np.random.permutation(T2)[:S]),
        "offs3": striped(np.random.permutation(T2)[:P]),
        "offs4": striped(np.random.permutation(T2)[:P]),
        "w1": (1.2 * n((K, H)) / s * u.T / np.sqrt(K)).astype(np.float32),
        "w2_words": w2_words, "w2_scales": w2_scales,
        "w3": (0.8 * n((K, H)) / s * u.T / np.sqrt(K)).astype(np.float32),
        "page0": (n((H, T2)) * u).astype(np.float32),
        "wgs": np.exp(0.3 * n((128, S))).astype(np.float32),
        "level": (0.8 * n(H) * u[:, 0]).astype(np.float32),
        "zone": (0.8 * n((H, P))).astype(np.float32),
        "wa": (0.8 * n((H, H)) / u * u.T / np.sqrt(H)).astype(np.float32),
        "wb_words": wb_words, "wb_scales": wb_scales,
        "base": (0.6 * n(H) * u[:, 0]).astype(np.float32),
        "wgo": np.exp(0.3 * n((128, P))).astype(np.float32),
    }

def reference(tab_words, tab_scales, offs, offs2, offs3, offs4, w1, w2_words, w2_scales, w3, page0, wgs, level, zone, wa, wb_words, wb_scales, base, wgo):
    v = unpack_weight(tab_words, tab_scales, "e4m3")[:, unstriped(offs)]
    heat = mxq(f64(w1), 0, "e4m3").T @ v
    turn = unpack_weight(w2_words, w2_scales, "e2m1").T @ v
    bed = mxq(f64(w3), 0, "e4m3").T @ v
    h = np.maximum(heat * np.tanh(turn), bed)
    page = f64(page0).copy()
    page[:, unstriped(offs2)] = np.tile(f64(wgs), (H // 128, 1)) * h
    x = page[:, unstriped(offs3)]
    xa = mxq(np.abs(x) + f64(level)[:, None], 0, "e4m3")
    xb = mxq(x * f64(zone), 0, "e4m3")
    y = mxq(f64(wa), 0, "e4m3").T @ xa + unpack_weight(wb_words, wb_scales, "e2m1").T @ xb
    y = y + f64(base)[:, None]
    page[:, unstriped(offs4)] = np.tile(f64(wgo), (H // 128, 1)) * y
    return page

@@ -1,0 +1,292 @@
+from contextlib import ExitStack
+
+import concourse.mybir as mybir
+
+K, H, T, S = 1024, 512, 2048, 1024
+
+F32 = mybir.dt.float32
+BF16 = mybir.dt.bfloat16
+I32 = mybir.dt.int32
+U32 = mybir.dt.uint32
+U16 = mybir.dt.uint16
+U8 = mybir.dt.uint8
+FP8X4 = mybir.dt.float8_e4m3fn_x4
+FP4X4 = mybir.dt.float4_e2m1fn_x4
+ACT = mybir.ActivationFunctionType
+ALU = mybir.AluOpType
+
+P = 128
+PACK = 4
+QUAD = 32
+N = 512
+HALVES = S // N
+PASSES = K // (P * PACK)
+LCOLS = N // 16
+
+FLOPS = 2 * (3 * K * H * S + 2 * H * H * S)
+
+
+def tile_list_grate_burnout_page_kernel(
+    tc, tab_words, tab_scales, offs, offs2, offs3, offs4, w1, w2_words, w2_scales, w3,
+    page0, wgs, level, zone, wa, wb_words, wb_scales, base, wgo, out,
+):
+    nc = tc.nc
+    with ExitStack() as ctx:
+        keep = ctx.enter_context(tc.tile_pool(name="keep", bufs=1))
+        ring = ctx.enter_context(tc.tile_pool(name="ring", bufs=5))
+        stage = ctx.enter_context(tc.tile_pool(name="stage", bufs=3))
+        psum = ctx.enter_context(tc.psum_pool(name="psum", bufs=8))
+
+        def kept(name, shape, dtype):
+            return keep.tile(shape, dtype, name=name, align_bytes=64)
+
+        def rows4(name):
+            return ring.tile([P, PACK, N], F32, name=name, tag="rows4")
+
+        def load_list(name, src):
+            lst = kept(name, [P, S // 16], U16)
+            nc.sync.dma_start(lst[:], src)
+            return lst
+
+        def load_dealt(dst, src):
+            for q in range(P // QUAD):
+                nc.sync.dma_start(dst[QUAD * q : QUAD * (q + 1)], src)
+
+        tab_sc = kept("tab_sc", [P, T], U8)
+        w2_sc_raw = kept("w2_sc_raw", [P, PASSES, H], U8)
+        v_sc1 = kept("v_sc1", [P, S], U8)
+        wb_sc_raw = kept("wb_sc_raw", [P, 1, H], U8)
+        nc.vector.memset(w2_sc_raw[:].bitcast(I32), 0)
+        nc.vector.memset(tab_sc[:].bitcast(I32), 0)
+        nc.vector.memset(v_sc1[:].bitcast(I32), 0)
+        nc.vector.memset(wb_sc_raw[:].bitcast(I32), 0)
+
+        tab_sc_in = kept("tab_sc_in", [P, T // 4], I32)
+        for q in range(4):
+            nc.sync.dma_start(
+                tab_sc_in[QUAD * q : QUAD * q + 8, :], tab_scales[:, 4 * q : 4 * q + 4, :].bitcast(I32)
+            )
+        idx = load_list("idx", offs)
+        tab_w = [kept("tab_w%d" % a, [P, T], U32) for a in range(PASSES)]
+
+        def load_tab(a):
+            nc.sync.dma_start(tab_w[a][:].bitcast(I32), tab_words[a].rearrange("p n i -> p (n i)").bitcast(I32))
+
+        load_tab(0)
+        w2_raw = kept("w2_raw", [P, PASSES, H], U16)
+        nc.sync.dma_start(w2_raw[:].bitcast(I32), w2_words.rearrange("a p n -> p a n").bitcast(I32))
+        for q in range(4):
+            nc.sync.dma_start(
+                w2_sc_raw[QUAD * q : QUAD * q + 4].bitcast(I32),
+                w2_scales[:, 4 * q : 4 * q + 4, :].rearrange("a r n -> r a n").bitcast(I32),
+            )
+        load_tab(1)
+
+        def load_weight(name, w, a):
+            raw = rows4(name) if name != "wa_raw" else keep.tile([P, PACK, N], F32, name=name, tag="wa_then_size")
+            nc.sync.dma_start(raw[:], w[P * PACK * a : P * PACK * (a + 1), :].rearrange("(p i) c -> p i c", i=PACK))
+            return raw
+
+        w1_raw = [load_weight("w1_raw", w1, a) for a in range(PASSES)]
+        w3_raw = [load_weight("w3_raw", w3, a) for a in range(PASSES)]
+
+        page_rows = page0.rearrange("(p t) c -> t p c", t=PACK)
+        out_rows = out.rearrange("(p t) c -> t p c", t=PACK)
+        page = [kept("page%d" % t, [P, T], F32) for t in range(PACK)]
+        wgs_rows = wgs.rearrange("(q t) j -> q t j", t=PACK)
+        wgs_first = kept("wgs_first", [P, 1, S], F32)
+        wgs_rest = kept("wgs_rest", [P, PACK - 1, S], F32)
+        nc.sync.dma_start(page[0][:], page_rows[0])
+        idx2 = load_list("idx2", offs2)
+        load_dealt(wgs_first, wgs_rows[:, 0:1, :])
+        idx3 = load_list("idx3", offs3)
+        level_sb = kept("level_sb", [P, PACK], F32)
+        nc.sync.dma_start(level_sb[:], level.rearrange("(p t) -> p t", t=PACK))
+        wa_raw = load_weight("wa_raw", wa, 0)
+        wb_raw = kept("wb_raw", [P, 1, H], U16)
+        nc.sync.dma_start(wb_raw[:].bitcast(I32), wb_words.rearrange("a p n -> p a n").bitcast(I32))
+        for q in range(4):
+            nc.sync.dma_start(
+                wb_sc_raw[QUAD * q : QUAD * q + 4].bitcast(I32),
+                wb_scales[:, 4 * q : 4 * q + 4, :].rearrange("a r n -> r a n").bitcast(I32),
+            )
+        nc.sync.dma_start(page[1][:], page_rows[1])
+        load_dealt(wgs_rest, wgs_rows[:, 1:PACK, :])
+        nc.sync.dma_start(page[2][:], page_rows[2])
+        zone_rows = zone.rearrange("(p t) j -> p t j", t=PACK)
+        zone_sb = []
+        for h in range(HALVES):
+            z = rows4("zone_sb")
+            nc.sync.dma_start(z[:], zone_rows[:, :, N * h : N * (h + 1)])
+            zone_sb.append(z)
+        nc.sync.dma_start(page[3][:], page_rows[3])
+        base_sb = kept("base_sb", [P, PACK], F32)
+        nc.sync.dma_start(base_sb[:], base.rearrange("(p t) -> p t", t=PACK))
+        idx4 = load_list("idx4", offs4)
+        wgo_rows = wgo.rearrange("(q t) j -> q t j", t=PACK)
+        wgo_sb = []
+        for h in range(HALVES):
+            g = rows4("wgo_sb")
+            load_dealt(g, wgo_rows[:, :, N * h : N * (h + 1)])
+            wgo_sb.append(g)
+
+        v_sc = kept("v_sc", [P, S], U8)
+        for q in range(4):
+            rows = slice(QUAD * q, QUAD * q + 8)
+            nc.vector.tensor_copy(tab_sc[rows, :].bitcast(I32), tab_sc_in[rows, :])
+        nc.vector.tensor_copy(v_sc[:], tab_sc[:].indirect(idx[:]))
+        for q in range(4):
+            nc.scalar.dma_start(
+                v_sc1[QUAD * q : QUAD * q + 4, :].bitcast(I32), v_sc[QUAD * q + 4 : QUAD * q + 8, :].bitcast(I32)
+            )
+        def deal_packed(name, raw, sc_raw, passes):
+            words = kept(name + "_w", [P, passes, H], U16)
+            scales = kept(name + "_sc", [P, passes, H], U8)
+            nc.scalar.copy(
+                words[:].rearrange("p a (t m) -> p a t m", t=PACK), raw[:].rearrange("p a (m t) -> p a t m", t=PACK)
+            )
+            nc.vector.tensor_copy(
+                scales[:].rearrange("p a (t m) -> p a t m", t=PACK), sc_raw[:].rearrange("p a (m t) -> p a t m", t=PACK)
+            )
+            return words, scales
+
+        w2_w, w2_sc = deal_packed("w2", w2_raw, w2_sc_raw, PASSES)
+        v_w = [kept("v_w%d" % a, [P, S], U32) for a in range(PASSES)]
+        for h in range(HALVES):
+            for a in range(PASSES):
+                nc.vector.tensor_copy(
+                    v_w[a][:, N * h : N * (h + 1)], tab_w[a][:].indirect(idx[:, LCOLS * h : LCOLS * (h + 1)])
+                )
+
+        def round_weight(raw, on_vector):
+            grouped = stage.tile([P, H * PACK], BF16, name="grouped", align_bytes=64)
+            dst = grouped[:].rearrange("p (t m i) -> p m i t", t=PACK, i=PACK)
+            src = raw[:].rearrange("p i (m t) -> p m i t", t=PACK)
+            if on_vector:
+                nc.vector.tensor_copy(dst, src)
+            else:
+                nc.scalar.copy(dst, src)
+            return grouped
+
+        def quantize(name, grouped):
+            codes = kept(name + "_q", [P, N], U32)
+            scales = kept(name + "_s", [P, N], U8)
+            nc.vector.quantize_mx(out=codes[:].bitcast(FP8X4), scales=scales[:], in_=grouped)
+            return codes, scales
+
+
+        def rows_of(t):
+            return slice(P * t, P * (t + 1))
+
+        def cols_of(h):
+            return slice(N * h, N * (h + 1))
+
+        def list_of(lst, h):
+            return lst[:, LCOLS * h : LCOLS * (h + 1)]
+
+        def first_product(name, weight, t, h):
+            acc = psum.tile([P, N], F32, name=name, tag="bank")
+            for a in range(PASSES):
+                codes, scales = weight[a]
+                nc.tensor.matmul_mx(
+                    out=acc[:],
+                    lhsT=codes[:, rows_of(t)].bitcast(FP8X4),
+                    lhsT_scale=scales[:, rows_of(t)],
+                    rhs=v_w[a][:, cols_of(h)].bitcast(FP8X4),
+                    rhs_scale=v_sc[4 * a : P, cols_of(h)],
+                    start=(a == 0),
+                    stop=(a == PASSES - 1),
+                )
+            return acc
+
+        feat = [kept("feat%d" % t, [P, S], F32) for t in range(PACK)]
+        for h in range(HALVES):
+            for t in range(PACK):
+                turn = psum.tile([P, N], F32, name="turn", tag="bank")
+                for a in range(PASSES):
+                    nc.tensor.matmul_mx(
+                        out=turn[:],
+                        lhsT=w2_w[:, a, rows_of(t)].bitcast(FP4X4),
+                        lhsT_scale=w2_sc[:, a, rows_of(t)],
+                        rhs=v_w[a][:, cols_of(h)].bitcast(FP8X4),
+                        rhs_scale=[v_sc, v_sc1][a][:, cols_of(h)],
+                        start=(a == 0),
+                        stop=(a == PASSES - 1),
+                    )
+                nc.scalar.activation(feat[t][:, cols_of(h)], turn[:], ACT.Tanh)
+
+        w1_q = []
+        for a in range(PASSES):
+            w1_q.append(quantize("w1_%d" % a, round_weight(w1_raw[a], True)[:]))
+        w3_g = [round_weight(w3_raw[a], False) for a in range(PASSES)]
+        for t in range(PACK):
+            for h in range(HALVES):
+                heat = first_product("heat", w1_q, t, h)
+                f = feat[t][:, cols_of(h)]
+                nc.vector.tensor_tensor(f, heat[:], f, ALU.mult)
+        w3_q = [quantize("w3_%d" % a, w3_g[a][:]) for a in range(PASSES)]
+
+        x = [kept("x%d" % h, [P, PACK, N], F32) for h in range(HALVES)]
+        xa = [kept("xa%d" % h, [P, N, PACK], BF16) for h in range(HALVES)]
+        xb = [kept("xb%d" % h, [P, N, PACK], BF16) for h in range(HALVES)]
+
+        def fetch(t, h):
+            nc.vector.tensor_copy(x[h][:, t, :], page[t][:].indirect(list_of(idx3, h)))
+            size = sizes[:, (HALVES * t + h) % PACK, :]
+            nc.scalar.activation(size, x[h][:, t, :], ACT.Abs)
+            nc.scalar.activation(xa[h][:, :, t], size, ACT.Identity, bias=level_sb[:, t : t + 1])
+
+        def make_xb(h):
+            nc.vector.tensor_tensor(
+                xb[h][:].rearrange("p (c i) t -> p c t i", i=4),
+                x[h][:].rearrange("p t (c i) -> p c t i", i=4),
+                zone_sb[h][:].rearrange("p t (c i) -> p c t i", i=4),
+                ALU.mult,
+            )
+
+        for t in range(PACK):
+            factor = wgs_first[:, 0, :] if t == 0 else wgs_rest[:, t - 1, :]
+            for h in range(HALVES):
+                bed = first_product("bed", w3_q, t, h)
+                f = feat[t][:, cols_of(h)]
+                nc.vector.tensor_tensor(f, bed[:], f, ALU.max)
+            nc.vector.tensor_tensor(page[t][:].indirect(idx2[:]), feat[t][:], factor, ALU.mult)
+            if t == 0:
+                wb_w, wb_sc = deal_packed("wb", wb_raw, wb_sc_raw, 1)
+                wa_q, wa_s = quantize("wa", round_weight(wa_raw, False)[:])
+                sizes = keep.tile([P, PACK, N], F32, name="sizes", tag="wa_then_size")
+            if t < PACK - 1:
+                for h in range(HALVES):
+                    fetch(t, h)
+
+        def quantize_x(h):
+            qb = quantize("xb%d" % h, xb[h][:].rearrange("p j t -> p (j t)"))
+            qa = quantize("xa%d" % h, xa[h][:].rearrange("p j t -> p (j t)"))
+            return qa, qb
+
+        def judge(t, h, qa, qb):
+            acc = psum.tile([P, N], F32, name="judged", tag="bank")
+            nc.tensor.matmul_mx(
+                out=acc[:], lhsT=wb_w[:, 0, rows_of(t)].bitcast(FP4X4), lhsT_scale=wb_sc[:, 0, rows_of(t)],
+                rhs=qb[0][:].bitcast(FP8X4), rhs_scale=qb[1][:], start=True, stop=False,
+            )
+            nc.tensor.matmul_mx(
+                out=acc[:], lhsT=wa_q[:, rows_of(t)].bitcast(FP8X4), lhsT_scale=wa_s[:, rows_of(t)],
+                rhs=qa[0][:].bitcast(FP8X4), rhs_scale=qa[1][:], start=False, stop=True,
+            )
+            y = stage.tile([P, N], F32, name="y")
+            nc.scalar.activation(y[:], acc[:], ACT.Identity, bias=base_sb[:, t : t + 1])
+            nc.vector.tensor_tensor(page[t][:].indirect(list_of(idx4, h)), y[:], wgo_sb[h][:, t, :], ALU.mult)
+
+        fetch(PACK - 1, 0)
+        make_xb(0)
+        fetch(PACK - 1, 1)
+        first = quantize_x(0)
+        make_xb(1)
+        judge(0, 0, *first)
+        second = quantize_x(1)
+        for t in range(1, PACK):
+            judge(t, 0, *first)
+        for t in range(PACK):
+            judge(t, 1, *second)
+            nc.sync.dma_start(out_rows[t], page[t][:])

@@ -1,6 +1,7 @@
 from contextlib import ExitStack
 
 import concourse.mybir as mybir
+from concourse.masks import make_identity
 
 K, H, T, S = 1024, 512, 2048, 1024
 
@@ -35,6 +36,7 @@ def tile_list_grate_burnout_page_kernel(
         keep = ctx.enter_context(tc.tile_pool(name="keep", bufs=1))
         ring = ctx.enter_context(tc.tile_pool(name="ring", bufs=5))
         stage = ctx.enter_context(tc.tile_pool(name="stage", bufs=3))
+        turning = ctx.enter_context(tc.tile_pool(name="turning", bufs=3))
         psum = ctx.enter_context(tc.psum_pool(name="psum", bufs=8))
 
         def kept(name, shape, dtype):
@@ -82,13 +84,15 @@ def tile_list_grate_burnout_page_kernel(
             )
         load_tab(1)
 
-        def load_weight(name, w, a):
-            raw = rows4(name) if name != "wa_raw" else keep.tile([P, PACK, N], F32, name=name, tag="wa_then_size")
+        def load_weight(name, w, a, raw=None):
+            if raw is None:
+                raw = rows4(name)
             nc.sync.dma_start(raw[:], w[P * PACK * a : P * PACK * (a + 1), :].rearrange("(p i) c -> p i c", i=PACK))
             return raw
 
         w1_raw = [load_weight("w1_raw", w1, a) for a in range(PASSES)]
-        w3_raw = [load_weight("w3_raw", w3, a) for a in range(PASSES)]
+        w3_last = keep.tile([P, PACK, N], F32, name="w3_last", tag="w3_then_feat")
+        w3_raw = [load_weight("w3_raw", w3, 0), load_weight("w3_raw", w3, 1, w3_last)]
 
         page_rows = page0.rearrange("(p t) c -> t p c", t=PACK)
         out_rows = out.rearrange("(p t) c -> t p c", t=PACK)
@@ -160,8 +164,8 @@ def tile_list_grate_burnout_page_kernel(
 
         def round_weight(raw, on_vector):
             grouped = stage.tile([P, H * PACK], BF16, name="grouped", align_bytes=64)
-            dst = grouped[:].rearrange("p (t m i) -> p m i t", t=PACK, i=PACK)
-            src = raw[:].rearrange("p i (m t) -> p m i t", t=PACK)
+            dst = grouped[:].rearrange("p (u v m i) -> p u m i v", u=2, v=2, i=PACK)
+            src = raw[:].rearrange("p i (m u v) -> p u m i v", u=2, v=2)
             if on_vector:
                 nc.vector.tensor_copy(dst, src)
             else:
@@ -199,32 +203,44 @@ def tile_list_grate_burnout_page_kernel(
                 )
             return acc
 
-        feat = [kept("feat%d" % t, [P, S], F32) for t in range(PACK)]
-        for h in range(HALVES):
-            for t in range(PACK):
-                turn = psum.tile([P, N], F32, name="turn", tag="bank")
-                for a in range(PASSES):
-                    nc.tensor.matmul_mx(
-                        out=turn[:],
-                        lhsT=w2_w[:, a, rows_of(t)].bitcast(FP4X4),
-                        lhsT_scale=w2_sc[:, a, rows_of(t)],
-                        rhs=v_w[a][:, cols_of(h)].bitcast(FP8X4),
-                        rhs_scale=[v_sc, v_sc1][a][:, cols_of(h)],
-                        start=(a == 0),
-                        stop=(a == PASSES - 1),
-                    )
-                nc.scalar.activation(feat[t][:, cols_of(h)], turn[:], ACT.Tanh)
+        def tanh_of_turn(t, h):
+            turn = psum.tile([P, N], F32, name="turn", tag="bank")
+            for a in range(PASSES):
+                nc.tensor.matmul_mx(
+                    out=turn[:],
+                    lhsT=w2_w[:, a, rows_of(t)].bitcast(FP4X4),
+                    lhsT_scale=w2_sc[:, a, rows_of(t)],
+                    rhs=v_w[a][:, cols_of(h)].bitcast(FP8X4),
+                    rhs_scale=[v_sc, v_sc1][a][:, cols_of(h)],
+                    start=(a == 0),
+                    stop=(a == PASSES - 1),
+                )
+            nc.scalar.activation(feat[t][:, cols_of(h)], turn[:], ACT.Tanh)
 
+        def times_heat(t, h):
+            heat = first_product("heat", w1_q, t, h)
+            f = feat[t][:, cols_of(h)]
+            nc.vector.tensor_tensor(f, heat[:], f, ALU.mult)
+
+        feat_early = kept("feat_early", [P, 2, S], F32)
+        feat = [feat_early[:, 0, :], feat_early[:, 1, :]]
+        for h in range(HALVES):
+            for t in range(2):
+                tanh_of_turn(t, h)
         w1_q = []
         for a in range(PASSES):
             w1_q.append(quantize("w1_%d" % a, round_weight(w1_raw[a], True)[:]))
         w3_g = [round_weight(w3_raw[a], False) for a in range(PASSES)]
-        for t in range(PACK):
+        for t in range(2):
             for h in range(HALVES):
-                heat = first_product("heat", w1_q, t, h)
-                f = feat[t][:, cols_of(h)]
-                nc.vector.tensor_tensor(f, heat[:], f, ALU.mult)
+                times_heat(t, h)
         w3_q = [quantize("w3_%d" % a, w3_g[a][:]) for a in range(PASSES)]
+        feat_late = keep.tile([P, 2, S], F32, name="feat_late", tag="w3_then_feat")
+        feat.extend([feat_late[:, 0, :], feat_late[:, 1, :]])
+        for t in range(2, PACK):
+            for h in range(HALVES):
+                tanh_of_turn(t, h)
+                times_heat(t, h)
 
         x = [kept("x%d" % h, [P, PACK, N], F32) for h in range(HALVES)]
         xa = [kept("xa%d" % h, [P, N, PACK], BF16) for h in range(HALVES)]
@@ -232,29 +248,64 @@ def tile_list_grate_burnout_page_kernel(
 
         def fetch(t, h):
             nc.vector.tensor_copy(x[h][:, t, :], page[t][:].indirect(list_of(idx3, h)))
-            size = sizes[:, (HALVES * t + h) % PACK, :]
-            nc.scalar.activation(size, x[h][:, t, :], ACT.Abs)
-            nc.scalar.activation(xa[h][:, :, t], size, ACT.Identity, bias=level_sb[:, t : t + 1])
+            size = turning.tile([P, N], F32, name="size", tag="bed_turned")
+            nc.scalar.activation(size[:], x[h][:, t, :], ACT.Abs)
+            nc.scalar.activation(xa[h][:, :, t], size[:], ACT.Identity, bias=level_sb[:, t : t + 1])
 
         def make_xb(h):
             nc.vector.tensor_tensor(
-                xb[h][:].rearrange("p (c i) t -> p c t i", i=4),
-                x[h][:].rearrange("p t (c i) -> p c t i", i=4),
-                zone_sb[h][:].rearrange("p t (c i) -> p c t i", i=4),
+                xb[h][:].rearrange("p (c i) t -> p c t i", i=2),
+                x[h][:].rearrange("p t (c i) -> p c t i", i=2),
+                zone_sb[h][:].rearrange("p t (c i) -> p c t i", i=2),
                 ALU.mult,
             )
 
-        for t in range(PACK):
-            factor = wgs_first[:, 0, :] if t == 0 else wgs_rest[:, t - 1, :]
-            for h in range(HALVES):
-                bed = first_product("bed", w3_q, t, h)
-                f = feat[t][:, cols_of(h)]
-                nc.vector.tensor_tensor(f, bed[:], f, ALU.max)
-            nc.vector.tensor_tensor(page[t][:].indirect(idx2[:]), feat[t][:], factor, ALU.mult)
+        ident = kept("ident", [P, P], F32)
+        make_identity(nc, ident[:])
+
+        def turned_sum(name, terms):
+            acc = psum.tile([P, N], F32, name=name, tag="bank")
+            for b in range(N // P):
+                for n, term in enumerate(terms):
+                    nc.tensor.matmul(
+                        acc[:, rows_of(b)], lhsT=term[:, rows_of(b)], rhs=ident[:], is_transpose=True,
+                        start=(n == 0), stop=(n == len(terms) - 1),
+                    )
+            return acc
+
+        def out_of_bank(name, acc, func, scale):
+            piece = turning.tile([P, N], F32, name=name)
+            nc.scalar.activation(piece[:], acc[:], func, scale=scale)
+            return piece
+
+        def larger(t, h):
+            bed = first_product("bed", w3_q, t, h)
+            f = feat[t][:, cols_of(h)]
             if t == 0:
-                wb_w, wb_sc = deal_packed("wb", wb_raw, wb_sc_raw, 1)
-                wa_q, wa_s = quantize("wa", round_weight(wa_raw, False)[:])
-                sizes = keep.tile([P, PACK, N], F32, name="sizes", tag="wa_then_size")
+                nc.vector.tensor_tensor(f, bed[:], f, ALU.max)
+                return
+            minus_bed = out_of_bank("minus_bed", bed, ACT.Copy, -1.0)
+            excess = out_of_bank("excess", turned_sum("diff", [f, minus_bed[:]]), ACT.Relu, 1.0)
+            bed_turned = out_of_bank("bed_turned", turned_sum("back", [minus_bed[:]]), ACT.Copy, -1.0)
+            nc.scalar.copy(f, turned_sum("total", [excess[:], bed_turned[:]])[:])
+
+        def put_first(t):
+            factor = wgs_first[:, 0, :] if t == 0 else wgs_rest[:, t - 1, :]
+            nc.vector.tensor_tensor(page[t][:].indirect(idx2[:]), feat[t], factor, ALU.mult)
+
+        for h in range(HALVES):
+            larger(0, h)
+        put_first(0)
+        for h in range(HALVES):
+            larger(1, h)
+        wb_w, wb_sc = deal_packed("wb", wb_raw, wb_sc_raw, 1)
+        wa_q, wa_s = quantize("wa", round_weight(wa_raw, False)[:])
+        for t in range(2, PACK):
+            for h in range(HALVES):
+                larger(t, h)
+        for t in range(PACK):
+            if t > 0:
+                put_first(t)
             if t < PACK - 1:
                 for h in range(HALVES):
                     fetch(t, h)
@@ -274,7 +325,7 @@ def tile_list_grate_burnout_page_kernel(
                 out=acc[:], lhsT=wa_q[:, rows_of(t)].bitcast(FP8X4), lhsT_scale=wa_s[:, rows_of(t)],
                 rhs=qa[0][:].bitcast(FP8X4), rhs_scale=qa[1][:], start=False, stop=True,
             )
-            y = stage.tile([P, N], F32, name="y")
+            y = turning.tile([P, N], F32, name="y", tag="excess")
             nc.scalar.activation(y[:], acc[:], ACT.Identity, bias=base_sb[:, t : t + 1])
             nc.vector.tensor_tensor(page[t][:].indirect(list_of(idx4, h)), y[:], wgo_sb[h][:, t, :], ALU.mult)
 

@@ -34,8 +34,8 @@ def tile_list_grate_burnout_page_kernel(
     nc = tc.nc
     with ExitStack() as ctx:
         keep = ctx.enter_context(tc.tile_pool(name="keep", bufs=1))
-        ring = ctx.enter_context(tc.tile_pool(name="ring", bufs=5))
-        stage = ctx.enter_context(tc.tile_pool(name="stage", bufs=3))
+        ring = ctx.enter_context(tc.tile_pool(name="ring", bufs=4))
+        stage = ctx.enter_context(tc.tile_pool(name="stage", bufs=4))
         turning = ctx.enter_context(tc.tile_pool(name="turning", bufs=3))
         psum = ctx.enter_context(tc.psum_pool(name="psum", bufs=8))
 
@@ -90,7 +90,8 @@ def tile_list_grate_burnout_page_kernel(
             nc.sync.dma_start(raw[:], w[P * PACK * a : P * PACK * (a + 1), :].rearrange("(p i) c -> p i c", i=PACK))
             return raw
 
-        w1_raw = [load_weight("w1_raw", w1, a) for a in range(PASSES)]
+        w1_first = keep.tile([P, PACK, N], F32, name="w1_first", tag="w1_then_feat")
+        w1_raw = [load_weight("w1_raw", w1, 0, w1_first), load_weight("w1_raw", w1, 1)]
         w3_last = keep.tile([P, PACK, N], F32, name="w3_last", tag="w3_then_feat")
         w3_raw = [load_weight("w3_raw", w3, 0), load_weight("w3_raw", w3, 1, w3_last)]
 
@@ -222,14 +223,13 @@ def tile_list_grate_burnout_page_kernel(
             f = feat[t][:, cols_of(h)]
             nc.vector.tensor_tensor(f, heat[:], f, ALU.mult)
 
-        feat_early = kept("feat_early", [P, 2, S], F32)
+        w1_g = [round_weight(w1_raw[a], a == 1) for a in range(PASSES)]
+        feat_early = keep.tile([P, 2, S], F32, name="feat_early", tag="w1_then_feat")
         feat = [feat_early[:, 0, :], feat_early[:, 1, :]]
         for h in range(HALVES):
             for t in range(2):
                 tanh_of_turn(t, h)
-        w1_q = []
-        for a in range(PASSES):
-            w1_q.append(quantize("w1_%d" % a, round_weight(w1_raw[a], True)[:]))
+        w1_q = [quantize("w1_%d" % a, w1_g[a][:]) for a in range(PASSES)]
         w3_g = [round_weight(w3_raw[a], False) for a in range(PASSES)]
         for t in range(2):
             for h in range(HALVES):
@@ -281,7 +281,7 @@ def tile_list_grate_burnout_page_kernel(
         def larger(t, h):
             bed = first_product("bed", w3_q, t, h)
             f = feat[t][:, cols_of(h)]
-            if t == 0:
+            if t < 2:
                 nc.vector.tensor_tensor(f, bed[:], f, ALU.max)
                 return
             minus_bed = out_of_bank("minus_bed", bed, ACT.Copy, -1.0)

from contextlib import ExitStack

import concourse.mybir as mybir
from concourse.masks import make_identity

K, H, T, S = 1024, 512, 2048, 1024

F32 = mybir.dt.float32
BF16 = mybir.dt.bfloat16
I32 = mybir.dt.int32
U32 = mybir.dt.uint32
U16 = mybir.dt.uint16
U8 = mybir.dt.uint8
FP8X4 = mybir.dt.float8_e4m3fn_x4
FP4X4 = mybir.dt.float4_e2m1fn_x4
ACT = mybir.ActivationFunctionType
ALU = mybir.AluOpType

P = 128
PACK = 4
QUAD = 32
N = 512
HALVES = S // N
PASSES = K // (P * PACK)
LCOLS = N // 16

FLOPS = 2 * (3 * K * H * S + 2 * H * H * S)


def tile_list_grate_burnout_page_kernel(
    tc, tab_words, tab_scales, offs, offs2, offs3, offs4, w1, w2_words, w2_scales, w3,
    page0, wgs, level, zone, wa, wb_words, wb_scales, base, wgo, out,
):
    nc = tc.nc
    with ExitStack() as ctx:
        keep = ctx.enter_context(tc.tile_pool(name="keep", bufs=1))
        ring = ctx.enter_context(tc.tile_pool(name="ring", bufs=4))
        stage = ctx.enter_context(tc.tile_pool(name="stage", bufs=4))
        turning = ctx.enter_context(tc.tile_pool(name="turning", bufs=3))
        psum = ctx.enter_context(tc.psum_pool(name="psum", bufs=8))

        def kept(name, shape, dtype):
            return keep.tile(shape, dtype, name=name, align_bytes=64)

        def rows4(name):
            return ring.tile([P, PACK, N], F32, name=name, tag="rows4")

        def load_list(name, src):
            lst = kept(name, [P, S // 16], U16)
            nc.sync.dma_start(lst[:], src)
            return lst

        def load_dealt(dst, src):
            for q in range(P // QUAD):
                nc.sync.dma_start(dst[QUAD * q : QUAD * (q + 1)], src)

        tab_sc = kept("tab_sc", [P, T], U8)
        w2_sc_raw = kept("w2_sc_raw", [P, PASSES, H], U8)
        v_sc1 = kept("v_sc1", [P, S], U8)
        wb_sc_raw = kept("wb_sc_raw", [P, 1, H], U8)
        nc.vector.memset(w2_sc_raw[:].bitcast(I32), 0)
        nc.vector.memset(tab_sc[:].bitcast(I32), 0)
        nc.vector.memset(v_sc1[:].bitcast(I32), 0)
        nc.vector.memset(wb_sc_raw[:].bitcast(I32), 0)

        tab_sc_in = kept("tab_sc_in", [P, T // 4], I32)
        for q in range(4):
            nc.sync.dma_start(
                tab_sc_in[QUAD * q : QUAD * q + 8, :], tab_scales[:, 4 * q : 4 * q + 4, :].bitcast(I32)
            )
        idx = load_list("idx", offs)
        tab_w = [kept("tab_w%d" % a, [P, T], U32) for a in range(PASSES)]

        def load_tab(a):
            nc.sync.dma_start(tab_w[a][:].bitcast(I32), tab_words[a].rearrange("p n i -> p (n i)").bitcast(I32))

        load_tab(0)
        w2_raw = kept("w2_raw", [P, PASSES, H], U16)
        nc.sync.dma_start(w2_raw[:].bitcast(I32), w2_words.rearrange("a p n -> p a n").bitcast(I32))
        for q in range(4):
            nc.sync.dma_start(
                w2_sc_raw[QUAD * q : QUAD * q + 4].bitcast(I32),
                w2_scales[:, 4 * q : 4 * q + 4, :].rearrange("a r n -> r a n").bitcast(I32),
            )
        load_tab(1)

        def load_weight(name, w, a, raw=None):
            if raw is None:
                raw = rows4(name)
            nc.sync.dma_start(raw[:], w[P * PACK * a : P * PACK * (a + 1), :].rearrange("(p i) c -> p i c", i=PACK))
            return raw

        w1_first = keep.tile([P, PACK, N], F32, name="w1_first", tag="w1_then_feat")
        w1_raw = [load_weight("w1_raw", w1, 0, w1_first), load_weight("w1_raw", w1, 1)]
        w3_last = keep.tile([P, PACK, N], F32, name="w3_last", tag="w3_then_feat")
        w3_raw = [load_weight("w3_raw", w3, 0), load_weight("w3_raw", w3, 1, w3_last)]

        page_rows = page0.rearrange("(p t) c -> t p c", t=PACK)
        out_rows = out.rearrange("(p t) c -> t p c", t=PACK)
        page = [kept("page%d" % t, [P, T], F32) for t in range(PACK)]
        wgs_rows = wgs.rearrange("(q t) j -> q t j", t=PACK)
        wgs_first = kept("wgs_first", [P, 1, S], F32)
        wgs_rest = kept("wgs_rest", [P, PACK - 1, S], F32)
        nc.sync.dma_start(page[0][:], page_rows[0])
        idx2 = load_list("idx2", offs2)
        load_dealt(wgs_first, wgs_rows[:, 0:1, :])
        idx3 = load_list("idx3", offs3)
        level_sb = kept("level_sb", [P, PACK], F32)
        nc.sync.dma_start(level_sb[:], level.rearrange("(p t) -> p t", t=PACK))
        wa_raw = load_weight("wa_raw", wa, 0)
        wb_raw = kept("wb_raw", [P, 1, H], U16)
        nc.sync.dma_start(wb_raw[:].bitcast(I32), wb_words.rearrange("a p n -> p a n").bitcast(I32))
        for q in range(4):
            nc.sync.dma_start(
                wb_sc_raw[QUAD * q : QUAD * q + 4].bitcast(I32),
                wb_scales[:, 4 * q : 4 * q + 4, :].rearrange("a r n -> r a n").bitcast(I32),
            )
        nc.sync.dma_start(page[1][:], page_rows[1])
        load_dealt(wgs_rest, wgs_rows[:, 1:PACK, :])
        nc.sync.dma_start(page[2][:], page_rows[2])
        zone_rows = zone.rearrange("(p t) j -> p t j", t=PACK)
        zone_sb = []
        for h in range(HALVES):
            z = rows4("zone_sb")
            nc.sync.dma_start(z[:], zone_rows[:, :, N * h : N * (h + 1)])
            zone_sb.append(z)
        nc.sync.dma_start(page[3][:], page_rows[3])
        base_sb = kept("base_sb", [P, PACK], F32)
        nc.sync.dma_start(base_sb[:], base.rearrange("(p t) -> p t", t=PACK))
        idx4 = load_list("idx4", offs4)
        wgo_rows = wgo.rearrange("(q t) j -> q t j", t=PACK)
        wgo_sb = []
        for h in range(HALVES):
            g = rows4("wgo_sb")
            load_dealt(g, wgo_rows[:, :, N * h : N * (h + 1)])
            wgo_sb.append(g)

        v_sc = kept("v_sc", [P, S], U8)
        for q in range(4):
            rows = slice(QUAD * q, QUAD * q + 8)
            nc.vector.tensor_copy(tab_sc[rows, :].bitcast(I32), tab_sc_in[rows, :])
        nc.vector.tensor_copy(v_sc[:], tab_sc[:].indirect(idx[:]))
        for q in range(4):
            nc.scalar.dma_start(
                v_sc1[QUAD * q : QUAD * q + 4, :].bitcast(I32), v_sc[QUAD * q + 4 : QUAD * q + 8, :].bitcast(I32)
            )
        def deal_packed(name, raw, sc_raw, passes):
            words = kept(name + "_w", [P, passes, H], U16)
            scales = kept(name + "_sc", [P, passes, H], U8)
            nc.scalar.copy(
                words[:].rearrange("p a (t m) -> p a t m", t=PACK), raw[:].rearrange("p a (m t) -> p a t m", t=PACK)
            )
            nc.vector.tensor_copy(
                scales[:].rearrange("p a (t m) -> p a t m", t=PACK), sc_raw[:].rearrange("p a (m t) -> p a t m", t=PACK)
            )
            return words, scales

        w2_w, w2_sc = deal_packed("w2", w2_raw, w2_sc_raw, PASSES)
        v_w = [kept("v_w%d" % a, [P, S], U32) for a in range(PASSES)]
        for h in range(HALVES):
            for a in range(PASSES):
                nc.vector.tensor_copy(
                    v_w[a][:, N * h : N * (h + 1)], tab_w[a][:].indirect(idx[:, LCOLS * h : LCOLS * (h + 1)])
                )

        def round_weight(raw, on_vector):
            grouped = stage.tile([P, H * PACK], BF16, name="grouped", align_bytes=64)
            dst = grouped[:].rearrange("p (u v m i) -> p u m i v", u=2, v=2, i=PACK)
            src = raw[:].rearrange("p i (m u v) -> p u m i v", u=2, v=2)
            if on_vector:
                nc.vector.tensor_copy(dst, src)
            else:
                nc.scalar.copy(dst, src)
            return grouped

        def quantize(name, grouped):
            codes = kept(name + "_q", [P, N], U32)
            scales = kept(name + "_s", [P, N], U8)
            nc.vector.quantize_mx(out=codes[:].bitcast(FP8X4), scales=scales[:], in_=grouped)
            return codes, scales


        def rows_of(t):
            return slice(P * t, P * (t + 1))

        def cols_of(h):
            return slice(N * h, N * (h + 1))

        def list_of(lst, h):
            return lst[:, LCOLS * h : LCOLS * (h + 1)]

        def first_product(name, weight, t, h):
            acc = psum.tile([P, N], F32, name=name, tag="bank")
            for a in range(PASSES):
                codes, scales = weight[a]
                nc.tensor.matmul_mx(
                    out=acc[:],
                    lhsT=codes[:, rows_of(t)].bitcast(FP8X4),
                    lhsT_scale=scales[:, rows_of(t)],
                    rhs=v_w[a][:, cols_of(h)].bitcast(FP8X4),
                    rhs_scale=v_sc[4 * a : P, cols_of(h)],
                    start=(a == 0),
                    stop=(a == PASSES - 1),
                )
            return acc

        def tanh_of_turn(t, h):
            turn = psum.tile([P, N], F32, name="turn", tag="bank")
            for a in range(PASSES):
                nc.tensor.matmul_mx(
                    out=turn[:],
                    lhsT=w2_w[:, a, rows_of(t)].bitcast(FP4X4),
                    lhsT_scale=w2_sc[:, a, rows_of(t)],
                    rhs=v_w[a][:, cols_of(h)].bitcast(FP8X4),
                    rhs_scale=[v_sc, v_sc1][a][:, cols_of(h)],
                    start=(a == 0),
                    stop=(a == PASSES - 1),
                )
            nc.scalar.activation(feat[t][:, cols_of(h)], turn[:], ACT.Tanh)

        def times_heat(t, h):
            heat = first_product("heat", w1_q, t, h)
            f = feat[t][:, cols_of(h)]
            nc.vector.tensor_tensor(f, heat[:], f, ALU.mult)

        w1_g = [round_weight(w1_raw[a], a == 1) for a in range(PASSES)]
        feat_early = keep.tile([P, 2, S], F32, name="feat_early", tag="w1_then_feat")
        feat = [feat_early[:, 0, :], feat_early[:, 1, :]]
        for h in range(HALVES):
            for t in range(2):
                tanh_of_turn(t, h)
        w1_q = [quantize("w1_%d" % a, w1_g[a][:]) for a in range(PASSES)]
        w3_g = [round_weight(w3_raw[a], False) for a in range(PASSES)]
        for t in range(2):
            for h in range(HALVES):
                times_heat(t, h)
        w3_q = [quantize("w3_%d" % a, w3_g[a][:]) for a in range(PASSES)]
        feat_late = keep.tile([P, 2, S], F32, name="feat_late", tag="w3_then_feat")
        feat.extend([feat_late[:, 0, :], feat_late[:, 1, :]])
        for t in range(2, PACK):
            for h in range(HALVES):
                tanh_of_turn(t, h)
                times_heat(t, h)

        x = [kept("x%d" % h, [P, PACK, N], F32) for h in range(HALVES)]
        xa = [kept("xa%d" % h, [P, N, PACK], BF16) for h in range(HALVES)]
        xb = [kept("xb%d" % h, [P, N, PACK], BF16) for h in range(HALVES)]

        def fetch(t, h):
            nc.vector.tensor_copy(x[h][:, t, :], page[t][:].indirect(list_of(idx3, h)))
            size = turning.tile([P, N], F32, name="size", tag="bed_turned")
            nc.scalar.activation(size[:], x[h][:, t, :], ACT.Abs)
            nc.scalar.activation(xa[h][:, :, t], size[:], ACT.Identity, bias=level_sb[:, t : t + 1])

        def make_xb(h):
            nc.vector.tensor_tensor(
                xb[h][:].rearrange("p (c i) t -> p c t i", i=2),
                x[h][:].rearrange("p t (c i) -> p c t i", i=2),
                zone_sb[h][:].rearrange("p t (c i) -> p c t i", i=2),
                ALU.mult,
            )

        ident = kept("ident", [P, P], F32)
        make_identity(nc, ident[:])

        def turned_sum(name, terms):
            acc = psum.tile([P, N], F32, name=name, tag="bank")
            for b in range(N // P):
                for n, term in enumerate(terms):
                    nc.tensor.matmul(
                        acc[:, rows_of(b)], lhsT=term[:, rows_of(b)], rhs=ident[:], is_transpose=True,
                        start=(n == 0), stop=(n == len(terms) - 1),
                    )
            return acc

        def out_of_bank(name, acc, func, scale):
            piece = turning.tile([P, N], F32, name=name)
            nc.scalar.activation(piece[:], acc[:], func, scale=scale)
            return piece

        def larger(t, h):
            bed = first_product("bed", w3_q, t, h)
            f = feat[t][:, cols_of(h)]
            if t < 2:
                nc.vector.tensor_tensor(f, bed[:], f, ALU.max)
                return
            minus_bed = out_of_bank("minus_bed", bed, ACT.Copy, -1.0)
            excess = out_of_bank("excess", turned_sum("diff", [f, minus_bed[:]]), ACT.Relu, 1.0)
            bed_turned = out_of_bank("bed_turned", turned_sum("back", [minus_bed[:]]), ACT.Copy, -1.0)
            nc.scalar.copy(f, turned_sum("total", [excess[:], bed_turned[:]])[:])

        def put_first(t):
            factor = wgs_first[:, 0, :] if t == 0 else wgs_rest[:, t - 1, :]
            nc.vector.tensor_tensor(page[t][:].indirect(idx2[:]), feat[t], factor, ALU.mult)

        for h in range(HALVES):
            larger(0, h)
        put_first(0)
        for h in range(HALVES):
            larger(1, h)
        wb_w, wb_sc = deal_packed("wb", wb_raw, wb_sc_raw, 1)
        wa_q, wa_s = quantize("wa", round_weight(wa_raw, False)[:])
        for t in range(2, PACK):
            for h in range(HALVES):
                larger(t, h)
        for t in range(PACK):
            if t > 0:
                put_first(t)
            if t < PACK - 1:
                for h in range(HALVES):
                    fetch(t, h)

        def quantize_x(h):
            qb = quantize("xb%d" % h, xb[h][:].rearrange("p j t -> p (j t)"))
            qa = quantize("xa%d" % h, xa[h][:].rearrange("p j t -> p (j t)"))
            return qa, qb

        def judge(t, h, qa, qb):
            acc = psum.tile([P, N], F32, name="judged", tag="bank")
            nc.tensor.matmul_mx(
                out=acc[:], lhsT=wb_w[:, 0, rows_of(t)].bitcast(FP4X4), lhsT_scale=wb_sc[:, 0, rows_of(t)],
                rhs=qb[0][:].bitcast(FP8X4), rhs_scale=qb[1][:], start=True, stop=False,
            )
            nc.tensor.matmul_mx(
                out=acc[:], lhsT=wa_q[:, rows_of(t)].bitcast(FP8X4), lhsT_scale=wa_s[:, rows_of(t)],
                rhs=qa[0][:].bitcast(FP8X4), rhs_scale=qa[1][:], start=False, stop=True,
            )
            y = turning.tile([P, N], F32, name="y", tag="excess")
            nc.scalar.activation(y[:], acc[:], ACT.Identity, bias=base_sb[:, t : t + 1])
            nc.vector.tensor_tensor(page[t][:].indirect(list_of(idx4, h)), y[:], wgo_sb[h][:, t, :], ALU.mult)

        fetch(PACK - 1, 0)
        make_xb(0)
        fetch(PACK - 1, 1)
        first = quantize_x(0)
        make_xb(1)
        judge(0, 0, *first)
        second = quantize_x(1)
        for t in range(1, PACK):
            judge(t, 0, *first)
        for t in range(PACK):
            judge(t, 1, *second)
            nc.sync.dma_start(out_rows[t], page[t][:])
